import numpy as np
import ml_dtypes


def mxq(x, axis, fmt="e4m3"):
    dtype, down = {"e4m3": (ml_dtypes.float8_e4m3fn, 7), "e5m2": (ml_dtypes.float8_e5m2, 14)}[fmt]
    v = np.moveaxis(np.asarray(x, np.float32).astype(ml_dtypes.bfloat16).astype(np.float64), axis, -1)
    blocks = v.reshape(v.shape[:-1] + (-1, 32))
    amax = np.abs(blocks).max(-1, keepdims=True)
    byte = np.maximum(np.where(amax > 0, np.frexp(amax)[1] - 1 + 127, 0) - down, 1)
    scale = np.exp2(byte - 127.0)
    codes = (blocks / scale).astype(np.float32).astype(dtype).astype(np.float64)
    return np.moveaxis((codes * scale).reshape(v.shape), -1, axis)


WIDE = False


def mx_kscale(k):
    if not WIDE:
        return np.ones(k)
    levels = np.array([30, -30])
    if k % 512:
        return np.exp2(np.random.permutation(np.resize(levels, k // 32))).repeat(32)
    a = np.empty((k // 512, 16))
    for p in range(k // 512):
        a[p, :8] = np.random.permutation(np.resize(levels, 8))
        for g in range(8):
            far = levels[np.abs(levels - a[p, g]) >= 10]
            a[p, g + 8] = far[np.random.randint(len(far))]
    return np.exp2(a.ravel()).repeat(32)


def f64(x):
    return np.asarray(x).astype(np.float64)


def striped(idx):
    return np.tile(np.asarray(idx).reshape(-1, 16).T, (8, 1)).astype(np.uint16)


def unstriped(offs):
    return offs[:16].T.reshape(-1).astype(np.int64)


E2M1 = np.array([0.0, 0.5, 1.0, 1.5, 2.0, 3.0, 4.0, 6.0, -0.0, -0.5, -1.0, -1.5, -2.0, -3.0, -4.0, -6.0])


def pack_weight(w, fmt):
    k, n = w.shape
    w = f64(np.asarray(w, np.float32).astype(ml_dtypes.bfloat16)).reshape(k // 32, 32, n)
    amax = np.abs(w).max(1)
    if fmt in ("e4m3", "e5m2"):
        byte = np.frexp(amax)[1] - 1 + 127 - (7 if fmt == "e4m3" else 14)
    else:
        mant, ex = np.frexp(amax / 6.0)
        byte = np.where(mant > 0.5, ex, ex - 1) + 127
    byte = np.clip(np.where(amax > 0, byte, 1), 1, 254)
    scaled = (w * np.exp2(127.0 - byte)[:, None, :]).reshape(k, n).astype(np.float32)
    by_word = np.ascontiguousarray(scaled.reshape(k // 512, 128, 4, n).transpose(0, 1, 3, 2))
    if fmt in ("e4m3", "e5m2"):
        words = by_word.astype(ml_dtypes.float8_e4m3fn if fmt == "e4m3" else ml_dtypes.float8_e5m2).view(np.uint8)
    else:
        c = by_word.astype(ml_dtypes.float4_e2m1fn).view(np.uint8) & 0xF
        words = (c[..., 0::2] | (c[..., 1::2] << 4)).reshape(k // 512, 128, 2 * n)
    return np.ascontiguousarray(words), np.ascontiguousarray(byte.astype(np.uint8).reshape(k // 512, 16, n))


def unpack_weight(words, scales, fmt):
    g, _, n = scales.shape
    words = np.ascontiguousarray(words).reshape(g, 128, n, -1)
    if fmt in ("e4m3", "e5m2"):
        vals = words.view(ml_dtypes.float8_e4m3fn if fmt == "e4m3" else ml_dtypes.float8_e5m2).astype(np.float64)
    else:
        nib = np.empty((g, 128, n, 4), np.uint8)
        nib[..., 0::2] = words & 0xF
        nib[..., 1::2] = words >> 4
        vals = E2M1[nib]
    vals = vals * np.repeat(np.exp2(scales.astype(np.float64) - 127.0), 8, axis=1)[..., None]
    return vals.transpose(0, 1, 3, 2).reshape(g * 512, n)


K, T, Z, J, R, O, N = 512, 1024, 1024, 256, 512, 128, 256


def setup_inputs():
    n = np.random.standard_normal
    idx = np.random.permutation(T)[:J]
    idx2 = np.random.permutation(Z)[:J]
    idx3 = np.random.permutation(J)[:O]
    idx4 = np.random.permutation(J)[:O]
    idx5 = np.random.permutation(J)[:O]
    idx6 = np.random.permutation(T)[:O]
    fk = mx_kscale(K)
    fr = mx_kscale(R)
    xtp = pack_weight(n((K, T)) / fk[:, None], "e4m3")
    xop = pack_weight(n((K, Z)) / fk[:, None], "e2m1")
    wp = pack_weight(n((K, R)) * 1 / np.sqrt(K) * fk[:, None] * fr, "e5m2")
    wbp = pack_weight(n((R, N)) * 1 / np.sqrt(R) / fr[:, None], "e5m2")
    wsp = pack_weight(n((K, N)) * 1 / np.sqrt(K) * fk[:, None], "e5m2")
    return {
        "xt_words": xtp[0],
        "xt_scales": xtp[1],
        "xo_words": xop[0],
        "xo_scales": xop[1],
        "w_words": wp[0],
        "w_scales": wp[1],
        "sa": (np.random.uniform(0.5, 1.6, (R, 1))).astype(np.float32),
        "sb": (np.random.uniform(0.5, 1.6, (R, 1))).astype(np.float32),
        "wb_words": wbp[0],
        "wb_scales": wbp[1],
        "ws_words": wsp[0],
        "ws_scales": wsp[1],
        "offs": striped(idx),
        "offs2": striped(idx2),
        "offs3": striped(idx3),
        "offs4": striped(idx4),
        "offs5": striped(idx5),
        "offs6": striped(idx6),
    }


def reference(xt_words, xt_scales, xo_words, xo_scales, w_words, w_scales, sa, sb, wb_words, wb_scales, ws_words, ws_scales, offs, offs2, offs3, offs4, offs5, offs6):
    idx = unstriped(offs)
    idx2 = unstriped(offs2)
    idx3 = unstriped(offs3)
    idx4 = unstriped(offs4)
    idx5 = unstriped(offs5)
    idx6 = unstriped(offs6)
    xtu = unpack_weight(xt_words, xt_scales, "e4m3")
    xou = unpack_weight(xo_words, xo_scales, "e2m1")
    wu = unpack_weight(w_words, w_scales, "e5m2")
    wbu = unpack_weight(wb_words, wb_scales, "e5m2")
    wsu = unpack_weight(ws_words, ws_scales, "e5m2")
    xtidxg = xtu[:, idx]
    a = wu.T @ xtidxg
    xoidx2g = xou[:, idx2]
    b = wu.T @ xoidx2g
    hid = np.maximum(a[:, idx3] * f64(sa), a[:, idx4]) - b[:, idx5] * f64(sb)
    hidq = mxq(hid, 0, "e4m3")
    xtidx6g = xtu[:, idx6]
    y = wbu.T @ hidq + wsu.T @ xtidx6g
    return y

@@ -1,0 +1,186 @@
+from contextlib import ExitStack
+
+import concourse.mybir as mybir
+
+K, T, Z, J, R, O, N = 512, 1024, 1024, 256, 512, 128, 256
+FLOPS = 2 * K * R * J * 2 + 2 * R * N * O + 2 * K * N * O
+
+F32 = mybir.dt.float32
+BF16 = mybir.dt.bfloat16
+I32 = mybir.dt.int32
+U32 = mybir.dt.uint32
+U16 = mybir.dt.uint16
+U8 = mybir.dt.uint8
+E4M3 = mybir.dt.float8_e4m3fn_x4
+E5M2 = mybir.dt.float8_e5m2_x4
+E2M1 = mybir.dt.float4_e2m1fn_x4
+ALU = mybir.AluOpType
+COPY = mybir.ActivationFunctionType.Copy
+P = 128
+A4_ON_SCALAR = 1
+
+
+def tile_list_overthird_oneforboth_further_plain_kernel(
+    tc, xt_words, xt_scales, xo_words, xo_scales, w_words, w_scales, sa, sb,
+    wb_words, wb_scales, ws_words, ws_scales, offs, offs2, offs3, offs4, offs5, offs6, out,
+):
+    nc = tc.nc
+    with ExitStack() as ctx:
+        sbuf = ctx.enter_context(tc.tile_pool(name="sbuf", bufs=1))
+        psum = ctx.enter_context(tc.psum_pool(name="psum", bufs=1))
+
+        def tile(name, shape, dtype):
+            return sbuf.tile(shape, dtype, name=name, align_bytes=64)
+
+        def load_list(name, src):
+            lst = tile(name, list(src.shape), U16)
+            nc.sync.dma_start(lst[:], src)
+            return lst
+
+        def load_words(queue, name, src, dtype, cols):
+            words = tile(name, [P, cols], dtype)
+            queue.dma_start(words[:].bitcast(I32), src.bitcast(I32))
+            return words
+
+        def fp8_words(src):
+            return src[0].rearrange("p n t -> p (n t)")
+
+        def load_plane_pairs(queue, stage, base, src, order):
+            rows = src[0].bitcast(I32).rearrange("(h q r) n -> q r h n", h=2, q=2)
+            for q in range(2):
+                dst = stage[base + 32 * q : base + 32 * q + 4, :].bitcast(I32).rearrange("p (h n) -> p h n", h=2)
+                queue.dma_start(dst, rows[q])
+
+        def load_plane(queue, dst, src):
+            for q in range(4):
+                queue.dma_start(dst[32 * q : 32 * q + 4, :].bitcast(I32), src[0, 4 * q : 4 * q + 4, :].bitcast(I32))
+
+        xo_pl = tile("xo_pl", [P, Z], U8)
+        xo_st = tile("xo_st", [P, 2 * Z], U8)
+        w_pl = tile("w_pl", [P, 2 * R], U8)
+        xt_pl = tile("xt_pl", [P, T], U8)
+        ws_pl = tile("ws_pl", [P, N], U8)
+        wb_pl = tile("wb_pl", [P, N], U8)
+        nc.vector.memset(xo_st[0:64, :].bitcast(I32), 0)
+        nc.vector.memset(w_pl[64:128, :].bitcast(I32), 0)
+        nc.vector.memset(xt_pl[:].bitcast(I32), 0)
+        nc.gpsimd.memset(ws_pl[:].bitcast(I32), 0)
+        nc.gpsimd.memset(wb_pl[:].bitcast(I32), 0)
+
+        l2 = load_list("l2", offs2)
+        xo_w = load_words(nc.sync, "xo_w", xo_words[0], U16, Z)
+        load_plane_pairs(nc.scalar, xo_st, 0, xo_scales, 0)
+        w_w = load_words(nc.sync, "w_w", fp8_words(w_words), U32, R)
+        load_plane_pairs(nc.scalar, w_pl, 64, w_scales, 0)
+        xt_w = load_words(nc.sync, "xt_w", fp8_words(xt_words), U32, T)
+        l1 = load_list("l1", offs)
+        load_plane(nc.scalar, xt_pl, xt_scales)
+        l5 = load_list("l5", offs5)
+        sb_t = tile("sb_t", [P, 4], F32)
+        nc.sync.dma_start(sb_t[:], sb.rearrange("(p t) o -> p (t o)", t=4))
+        l6 = load_list("l6", offs6)
+        l3 = load_list("l3", offs3)
+        sa_t = tile("sa_t", [P, 4], F32)
+        nc.sync.dma_start(sa_t[:], sa.rearrange("(p t) o -> p (t o)", t=4))
+        l4 = load_list("l4", offs4)
+        ws_w = load_words(nc.sync, "ws_w", fp8_words(ws_words), U32, N)
+        load_plane(nc.sync, ws_pl, ws_scales)
+        wb_w = load_words(nc.sync, "wb_w", fp8_words(wb_words), U32, N)
+        load_plane(nc.sync, wb_pl, wb_scales)
+
+        nc.vector.tensor_copy(xo_pl[0:64, :].bitcast(I32), xo_st[0:64, 0:Z].bitcast(I32))
+        nc.vector.tensor_copy(xo_pl[64:128, :].bitcast(I32), xo_st[0:64, Z : 2 * Z].bitcast(I32))
+        nc.vector.tensor_copy(w_pl[0:64, R : 2 * R].bitcast(I32), w_pl[64:128, 0:R].bitcast(I32))
+        wp_pl = tile("wp_pl", [P, R], U8)
+        nc.vector.tensor_copy(
+            wp_pl[:].rearrange("p (t m) -> p t m", t=4), w_pl[:, R : 2 * R].rearrange("p (m t) -> p t m", t=4)
+        )
+        wp_w = tile("wp_w", [P, R], U32)
+        nc.scalar.copy(
+            wp_w[:].rearrange("p (t c i) -> p c t i", t=4, i=4), w_w[:].rearrange("p (c i t) -> p c t i", t=4, i=4)
+        )
+
+        xo_g = tile("xo_g", [P, J], U16)
+        xo_gs = tile("xo_gs", [P, J], U8)
+        nc.vector.tensor_copy(xo_g[:], xo_w[:].indirect(l2[:]))
+        nc.vector.tensor_copy(xo_gs[:], xo_pl[:].indirect(l2[:]))
+        xt_g = tile("xt_g", [P, J], U32)
+        xt_gs = tile("xt_gs", [P, J], U8)
+        nc.vector.tensor_copy(xt_g[:], xt_w[:].indirect(l1[:]))
+        nc.vector.tensor_copy(xt_gs[:], xt_pl[:].indirect(l1[:]))
+        x6_g = tile("x6_g", [P, O], U32)
+        x6_gs = tile("x6_gs", [P, O], U8)
+        nc.vector.tensor_copy(x6_g[:], xt_w[:].indirect(l6[:]))
+        nc.vector.tensor_copy(x6_gs[:], xt_pl[:].indirect(l6[:]))
+
+        def first_stage(bank, t, codes, scales):
+            acc = psum.tile([P, J], F32, name="acc", tag=f"bank{bank}")
+            cols = slice(t * P, (t + 1) * P)
+            nc.tensor.matmul_mx(
+                out=acc[:], lhsT=wp_w[:, cols].bitcast(E5M2), lhsT_scale=wp_pl[:, cols],
+                rhs=codes, rhs_scale=scales, start=True, stop=True,
+            )
+            return acc
+
+        b_ps = [first_stage(t, t, xo_g[:].bitcast(E2M1), xo_gs[:]) for t in range(4)]
+        a_ps = [first_stage(4 + t, t, xt_g[:].bitcast(E4M3), xt_gs[:]) for t in range(4)]
+
+        b_sb = [tile(f"b_sb{t}", [P, J], F32) for t in range(4)]
+        a_sb = [tile(f"a_sb{t}", [P, J], F32) for t in range(4)]
+        a3 = tile("a3", [P, 4, O], F32)
+        a4 = tile("a4", [P, 4, O], F32)
+        b5 = tile("b5", [P, 4, O], F32)
+        top = tile("top", [P, 4, O], F32)
+
+        def look(dst, window, lst, scale):
+            nc.scalar.activation(out=dst, in_=window[:].indirect(lst[:]), func=COPY, scale=scale)
+
+        for t in range(5):
+            if t < 4:
+                nc.scalar.activation(out=b_sb[t][:], in_=b_ps[t][:], func=COPY)
+            if t > 0:
+                look(b5[:, t - 1, :], b_sb[t - 1], l5, sb_t[:, t - 1 : t])
+
+        y_ps = [psum.tile([P, O], F32, name="y_ps", tag=f"bank{h}") for h in range(2)]
+        for h in range(2):
+            cols = slice(h * P, (h + 1) * P)
+            nc.tensor.matmul_mx(
+                out=y_ps[h][:], lhsT=ws_w[:, cols].bitcast(E5M2), lhsT_scale=ws_pl[:, cols],
+                rhs=x6_g[:].bitcast(E4M3), rhs_scale=x6_gs[:], start=True, stop=False,
+            )
+
+        for t in range(5):
+            if t < 4:
+                nc.vector.tensor_copy(a_sb[t][:], a_ps[t][:])
+            if t > 0:
+                s = t - 1
+                look(a3[:, s, :], a_sb[s], l3, sa_t[:, s : s + 1])
+                if s < 4 - A4_ON_SCALAR:
+                    nc.vector.tensor_copy(a4[:, s, :], a_sb[s][:].indirect(l4[:]))
+        for s in range(4 - A4_ON_SCALAR, 4):
+            nc.scalar.activation(out=a4[:, s, :], in_=a_sb[s][:].indirect(l4[:]), func=COPY)
+        nc.vector.tensor_tensor(top[:, 0:3, :], a3[:, 0:3, :], a4[:, 0:3, :], ALU.max)
+        nc.vector.tensor_tensor(top[:, 3, :], a3[:, 3, :], a4[:, 3, :], ALU.max)
+
+        hid = tile("hid", [P, O, 4], BF16)
+        nc.vector.tensor_tensor(
+            hid[:].rearrange("p (c i) t -> p c t i", i=4),
+            top[:].rearrange("p t (c i) -> p c t i", i=4),
+            b5[:].rearrange("p t (c i) -> p c t i", i=4),
+            ALU.subtract,
+        )
+        hid_q = tile("hid_q", [P, O], U32)
+        hid_s = tile("hid_s", [P, O], U8)
+        nc.vector.quantize_mx(out=hid_q[:].bitcast(E4M3), scales=hid_s[:], in_=hid[:].rearrange("p o t -> p (o t)"))
+
+        y_sb = [tile(f"y{h}", [P, O], F32) for h in range(2)]
+        for h in range(2):
+            cols = slice(h * P, (h + 1) * P)
+            nc.tensor.matmul_mx(
+                out=y_ps[h][:], lhsT=wb_w[:, cols].bitcast(E5M2), lhsT_scale=wb_pl[:, cols],
+                rhs=hid_q[:].bitcast(E4M3), rhs_scale=hid_s[:], start=False, stop=True,
+            )
+        nc.vector.tensor_copy(y_sb[0][:], y_ps[0][:])
+        nc.sync.dma_start(out[0:P, :], y_sb[0][:])
+        nc.scalar.copy(y_sb[1][:], y_ps[1][:])
+        nc.scalar.dma_start(out[P : 2 * P, :], y_sb[1][:])

@@ -29,8 +29,8 @@ def tile_list_overthird_oneforboth_further_plain_kernel(
         sbuf = ctx.enter_context(tc.tile_pool(name="sbuf", bufs=1))
         psum = ctx.enter_context(tc.psum_pool(name="psum", bufs=1))
 
-        def tile(name, shape, dtype):
-            return sbuf.tile(shape, dtype, name=name, align_bytes=64)
+        def tile(name, shape, dtype, tag=None):
+            return sbuf.tile(shape, dtype, name=name, tag=tag or name, align_bytes=64)
 
         def load_list(name, src):
             lst = tile(name, list(src.shape), U16)
@@ -45,72 +45,70 @@ def tile_list_overthird_oneforboth_further_plain_kernel(
         def fp8_words(src):
             return src[0].rearrange("p n t -> p (n t)")
 
-        def load_plane_pairs(queue, stage, base, src, order):
-            rows = src[0].bitcast(I32).rearrange("(h q r) n -> q r h n", h=2, q=2)
-            for q in range(2):
-                dst = stage[base + 32 * q : base + 32 * q + 4, :].bitcast(I32).rearrange("p (h n) -> p h n", h=2)
-                queue.dma_start(dst, rows[q])
-
         def load_plane(queue, dst, src):
             for q in range(4):
                 queue.dma_start(dst[32 * q : 32 * q + 4, :].bitcast(I32), src[0, 4 * q : 4 * q + 4, :].bitcast(I32))
 
         xo_pl = tile("xo_pl", [P, Z], U8)
-        xo_st = tile("xo_st", [P, 2 * Z], U8)
-        w_pl = tile("w_pl", [P, 2 * R], U8)
+        w_st = tile("w_st", [4, 4, R // 4], I32)
+        w_pl = tile("w_pl", [P, R], U8)
         xt_pl = tile("xt_pl", [P, T], U8)
-        ws_pl = tile("ws_pl", [P, N], U8)
-        wb_pl = tile("wb_pl", [P, N], U8)
-        nc.vector.memset(xo_st[0:64, :].bitcast(I32), 0)
-        nc.vector.memset(w_pl[64:128, :].bitcast(I32), 0)
+        nc.vector.memset(xo_pl[:].bitcast(I32), 0)
         nc.vector.memset(xt_pl[:].bitcast(I32), 0)
-        nc.gpsimd.memset(ws_pl[:].bitcast(I32), 0)
-        nc.gpsimd.memset(wb_pl[:].bitcast(I32), 0)
+        nc.vector.memset(w_pl[:].bitcast(I32), 0)
 
+        xt_w = load_words(nc.gpsimd, "xt_w", fp8_words(xt_words), U32, T)
+        nc.scalar.dma_start(w_st[:], w_scales[0].bitcast(I32).rearrange("(q r) n -> r q n", q=4))
+        xo_w = load_words(nc.scalar, "xo_w", xo_words[0], U16, Z)
+        w_w = load_words(nc.scalar, "w_w", fp8_words(w_words), U32, R)
         l2 = load_list("l2", offs2)
-        xo_w = load_words(nc.sync, "xo_w", xo_words[0], U16, Z)
-        load_plane_pairs(nc.scalar, xo_st, 0, xo_scales, 0)
-        w_w = load_words(nc.sync, "w_w", fp8_words(w_words), U32, R)
-        load_plane_pairs(nc.scalar, w_pl, 64, w_scales, 0)
-        xt_w = load_words(nc.sync, "xt_w", fp8_words(xt_words), U32, T)
         l1 = load_list("l1", offs)
-        load_plane(nc.scalar, xt_pl, xt_scales)
         l5 = load_list("l5", offs5)
-        sb_t = tile("sb_t", [P, 4], F32)
-        nc.sync.dma_start(sb_t[:], sb.rearrange("(p t) o -> p (t o)", t=4))
         l6 = load_list("l6", offs6)
         l3 = load_list("l3", offs3)
-        sa_t = tile("sa_t", [P, 4], F32)
-        nc.sync.dma_start(sa_t[:], sa.rearrange("(p t) o -> p (t o)", t=4))
         l4 = load_list("l4", offs4)
-        ws_w = load_words(nc.sync, "ws_w", fp8_words(ws_words), U32, N)
-        load_plane(nc.sync, ws_pl, ws_scales)
-        wb_w = load_words(nc.sync, "wb_w", fp8_words(wb_words), U32, N)
-        load_plane(nc.sync, wb_pl, wb_scales)
+        load_plane(nc.sync, xo_pl, xo_scales)
+        load_plane(nc.sync, xt_pl, xt_scales)
 
-        nc.vector.tensor_copy(xo_pl[0:64, :].bitcast(I32), xo_st[0:64, 0:Z].bitcast(I32))
-        nc.vector.tensor_copy(xo_pl[64:128, :].bitcast(I32), xo_st[0:64, Z : 2 * Z].bitcast(I32))
-        nc.vector.tensor_copy(w_pl[0:64, R : 2 * R].bitcast(I32), w_pl[64:128, 0:R].bitcast(I32))
+        for q in range(4):
+            nc.vector.tensor_copy(w_pl[32 * q : 32 * q + 4, :].bitcast(I32), w_st[:, q, :])
         wp_pl = tile("wp_pl", [P, R], U8)
         nc.vector.tensor_copy(
-            wp_pl[:].rearrange("p (t m) -> p t m", t=4), w_pl[:, R : 2 * R].rearrange("p (m t) -> p t m", t=4)
+            wp_pl[:].rearrange("p (t m) -> p t m", t=4), w_pl[:].rearrange("p (m t) -> p t m", t=4)
         )
         wp_w = tile("wp_w", [P, R], U32)
         nc.scalar.copy(
             wp_w[:].rearrange("p (t c i) -> p c t i", t=4, i=4), w_w[:].rearrange("p (c i t) -> p c t i", t=4, i=4)
         )
+        gains = tile("gains", [P, 16], F32, tag="w_st")
+        sb_t = gains[:, 0:4]
+        sa_t = gains[:, 8:12]
+        nc.sync.dma_start(sb_t, sb.rearrange("(p t) o -> p (t o)", t=4))
+        nc.sync.dma_start(sa_t, sa.rearrange("(p t) o -> p (t o)", t=4))
+        out_w = tile("out_w", [P, 2 * N], U32, tag="w_w")
+        ws_w = out_w[:, 0:N]
+        wb_w = out_w[:, N : 2 * N]
+        nc.sync.dma_start(ws_w.bitcast(I32), fp8_words(ws_words).bitcast(I32))
+        nc.sync.dma_start(wb_w.bitcast(I32), fp8_words(wb_words).bitcast(I32))
+        out_pl = tile("out_pl", [P, 2 * N], U8, tag="w_pl")
+        ws_pl = out_pl[:, 0:N]
+        wb_pl = out_pl[:, N : 2 * N]
+        nc.vector.memset(out_pl[:].bitcast(I32), 0)
+        load_plane(nc.sync, ws_pl, ws_scales)
+        load_plane(nc.sync, wb_pl, wb_scales)
 
         xo_g = tile("xo_g", [P, J], U16)
         xo_gs = tile("xo_gs", [P, J], U8)
         nc.vector.tensor_copy(xo_g[:], xo_w[:].indirect(l2[:]))
         nc.vector.tensor_copy(xo_gs[:], xo_pl[:].indirect(l2[:]))
-        xt_g = tile("xt_g", [P, J], U32)
+        picked = tile("picked", [P, J + O], U32, tag="xo_pl")
+        xt_g = picked[:, 0:J]
+        x6_g = picked[:, J : J + O]
         xt_gs = tile("xt_gs", [P, J], U8)
-        nc.vector.tensor_copy(xt_g[:], xt_w[:].indirect(l1[:]))
-        nc.vector.tensor_copy(xt_gs[:], xt_pl[:].indirect(l1[:]))
-        x6_g = tile("x6_g", [P, O], U32)
         x6_gs = tile("x6_gs", [P, O], U8)
-        nc.vector.tensor_copy(x6_g[:], xt_w[:].indirect(l6[:]))
+        nc.vector.tensor_copy(xt_g, xt_w[:].indirect(l1[:]))
+        nc.vector.tensor_copy(xt_gs[:], xt_pl[:].indirect(l1[:]))
+        nc.vector.tensor_copy(x6_g, xt_w[:].indirect(l6[:]))
         nc.vector.tensor_copy(x6_gs[:], xt_pl[:].indirect(l6[:]))
 
         def first_stage(bank, t, codes, scales):
@@ -123,9 +121,9 @@ def tile_list_overthird_oneforboth_further_plain_kernel(
             return acc
 
         b_ps = [first_stage(t, t, xo_g[:].bitcast(E2M1), xo_gs[:]) for t in range(4)]
-        a_ps = [first_stage(4 + t, t, xt_g[:].bitcast(E4M3), xt_gs[:]) for t in range(4)]
+        a_ps = [first_stage(4 + t, t, xt_g.bitcast(E4M3), xt_gs[:]) for t in range(4)]
 
-        b_sb = [tile(f"b_sb{t}", [P, J], F32) for t in range(4)]
+        b_sb = [tile(f"b_sb{t}", [P, J], F32) for t in range(3)]
         a_sb = [tile(f"a_sb{t}", [P, J], F32) for t in range(4)]
         a3 = tile("a3", [P, 4, O], F32)
         a4 = tile("a4", [P, 4, O], F32)
@@ -135,8 +133,8 @@ def tile_list_overthird_oneforboth_further_plain_kernel(
         def look(dst, window, lst, scale):
             nc.scalar.activation(out=dst, in_=window[:].indirect(lst[:]), func=COPY, scale=scale)
 
-        for t in range(5):
-            if t < 4:
+        for t in range(4):
+            if t < 3:
                 nc.scalar.activation(out=b_sb[t][:], in_=b_ps[t][:], func=COPY)
             if t > 0:
                 look(b5[:, t - 1, :], b_sb[t - 1], l5, sb_t[:, t - 1 : t])
@@ -146,32 +144,37 @@ def tile_list_overthird_oneforboth_further_plain_kernel(
             cols = slice(h * P, (h + 1) * P)
             nc.tensor.matmul_mx(
                 out=y_ps[h][:], lhsT=ws_w[:, cols].bitcast(E5M2), lhsT_scale=ws_pl[:, cols],
-                rhs=x6_g[:].bitcast(E4M3), rhs_scale=x6_gs[:], start=True, stop=False,
+                rhs=x6_g.bitcast(E4M3), rhs_scale=x6_gs[:], start=True, stop=False,
             )
 
-        for t in range(5):
-            if t < 4:
-                nc.vector.tensor_copy(a_sb[t][:], a_ps[t][:])
-            if t > 0:
-                s = t - 1
-                look(a3[:, s, :], a_sb[s], l3, sa_t[:, s : s + 1])
-                if s < 4 - A4_ON_SCALAR:
-                    nc.vector.tensor_copy(a4[:, s, :], a_sb[s][:].indirect(l4[:]))
-        for s in range(4 - A4_ON_SCALAR, 4):
-            nc.scalar.activation(out=a4[:, s, :], in_=a_sb[s][:].indirect(l4[:]), func=COPY)
+        for t in range(4):
+            nc.vector.tensor_copy(a_sb[t][:], a_ps[t][:])
+            look(a3[:, t, :], a_sb[t], l3, sa_t[:, t : t + 1])
+        for t in range(3):
+            nc.vector.tensor_copy(a4[:, t, :], a_sb[t][:].indirect(l4[:]))
+        b_last = tile("b_last", [P, J], F32, tag="a_sb0")
+        nc.scalar.activation(out=b_last[:], in_=b_ps[3][:], func=COPY)
+        nc.scalar.activation(out=a4[:, 3, :], in_=a_sb[3][:].indirect(l4[:]), func=COPY)
+        look(b5[:, 3, :], b_last, l5, sb_t[:, 3:4])
         nc.vector.tensor_tensor(top[:, 0:3, :], a3[:, 0:3, :], a4[:, 0:3, :], ALU.max)
         nc.vector.tensor_tensor(top[:, 3, :], a3[:, 3, :], a4[:, 3, :], ALU.max)
 
         hid = tile("hid", [P, O, 4], BF16)
-        nc.vector.tensor_tensor(
-            hid[:].rearrange("p (c i) t -> p c t i", i=4),
-            top[:].rearrange("p t (c i) -> p c t i", i=4),
-            b5[:].rearrange("p t (c i) -> p c t i", i=4),
-            ALU.subtract,
-        )
         hid_q = tile("hid_q", [P, O], U32)
         hid_s = tile("hid_s", [P, O], U8)
-        nc.vector.quantize_mx(out=hid_q[:].bitcast(E4M3), scales=hid_s[:], in_=hid[:].rearrange("p o t -> p (o t)"))
+        halves = [slice(0, O // 2), slice(O // 2, O)]
+        for cols in halves:
+            nc.vector.tensor_tensor(
+                hid[:, cols, :].rearrange("p (c i) t -> p c t i", i=4),
+                top[:, :, cols].rearrange("p t (c i) -> p c t i", i=4),
+                b5[:, :, cols].rearrange("p t (c i) -> p c t i", i=4),
+                ALU.subtract,
+            )
+        for cols in halves:
+            nc.vector.quantize_mx(
+                out=hid_q[:, cols].bitcast(E4M3), scales=hid_s[:, cols],
+                in_=hid[:, cols, :].rearrange("p o t -> p (o t)"),
+            )
 
         y_sb = [tile(f"y{h}", [P, O], F32) for h in range(2)]
         for h in range(2):

@@ -16,8 +16,12 @@ E5M2 = mybir.dt.float8_e5m2_x4
 E2M1 = mybir.dt.float4_e2m1fn_x4
 ALU = mybir.AluOpType
 COPY = mybir.ActivationFunctionType.Copy
+
 P = 128
-A4_ON_SCALAR = 1
+PACK = 4
+QUADS = 4
+LAST = PACK - 1
+RUN = 4
 
 
 def tile_list_overthird_oneforboth_further_plain_kernel(
@@ -45,145 +49,148 @@ def tile_list_overthird_oneforboth_further_plain_kernel(
         def fp8_words(src):
             return src[0].rearrange("p n t -> p (n t)")
 
-        def load_plane(queue, dst, src):
-            for q in range(4):
-                queue.dma_start(dst[32 * q : 32 * q + 4, :].bitcast(I32), src[0, 4 * q : 4 * q + 4, :].bitcast(I32))
+        def load_plane(plane, src):
+            for q in range(QUADS):
+                rows = src[0, 4 * q : 4 * q + 4, :]
+                nc.sync.dma_start(plane[32 * q : 32 * q + 4, :].bitcast(I32), rows.bitcast(I32))
 
-        xo_pl = tile("xo_pl", [P, Z], U8)
-        w_st = tile("w_st", [4, 4, R // 4], I32)
-        w_pl = tile("w_pl", [P, R], U8)
-        xt_pl = tile("xt_pl", [P, T], U8)
-        nc.vector.memset(xo_pl[:].bitcast(I32), 0)
-        nc.vector.memset(xt_pl[:].bitcast(I32), 0)
-        nc.vector.memset(w_pl[:].bitcast(I32), 0)
+        xo_plane = tile("xo_plane", [P, Z], U8)
+        w_rows = tile("w_rows", [4, QUADS, R // 4], I32)
+        w_plane = tile("w_plane", [P, R], U8)
+        xt_plane = tile("xt_plane", [P, T], U8)
+        nc.vector.memset(xo_plane[:].bitcast(I32), 0)
+        nc.vector.memset(xt_plane[:].bitcast(I32), 0)
+        nc.vector.memset(w_plane[:].bitcast(I32), 0)
 
-        xt_w = load_words(nc.gpsimd, "xt_w", fp8_words(xt_words), U32, T)
-        nc.scalar.dma_start(w_st[:], w_scales[0].bitcast(I32).rearrange("(q r) n -> r q n", q=4))
-        xo_w = load_words(nc.scalar, "xo_w", xo_words[0], U16, Z)
-        w_w = load_words(nc.scalar, "w_w", fp8_words(w_words), U32, R)
-        l2 = load_list("l2", offs2)
-        l1 = load_list("l1", offs)
-        l5 = load_list("l5", offs5)
-        l6 = load_list("l6", offs6)
-        l3 = load_list("l3", offs3)
-        l4 = load_list("l4", offs4)
-        load_plane(nc.sync, xo_pl, xo_scales)
-        load_plane(nc.sync, xt_pl, xt_scales)
+        w_raw = load_words(nc.gpsimd, "w_raw", fp8_words(w_words), U32, R)
+        xt_table = load_words(nc.gpsimd, "xt_table", fp8_words(xt_words), U32, T)
+        nc.scalar.dma_start(w_rows[:], w_scales[0].bitcast(I32).rearrange("(q i) n -> i q n", q=QUADS))
+        list2 = load_list("list2", offs2)
+        list1 = load_list("list1", offs)
+        list5 = load_list("list5", offs5)
+        xo_table = load_words(nc.sync, "xo_table", xo_words[0], U16, Z)
+        list6 = load_list("list6", offs6)
+        list3 = load_list("list3", offs3)
+        list4 = load_list("list4", offs4)
+        load_plane(xo_plane, xo_scales)
+        load_plane(xt_plane, xt_scales)
 
-        for q in range(4):
-            nc.vector.tensor_copy(w_pl[32 * q : 32 * q + 4, :].bitcast(I32), w_st[:, q, :])
-        wp_pl = tile("wp_pl", [P, R], U8)
+        for q in range(QUADS):
+            nc.vector.tensor_copy(w_plane[32 * q : 32 * q + 4, :].bitcast(I32), w_rows[:, q, :])
+        w_dealt_plane = tile("w_dealt_plane", [P, R], U8)
         nc.vector.tensor_copy(
-            wp_pl[:].rearrange("p (t m) -> p t m", t=4), w_pl[:].rearrange("p (m t) -> p t m", t=4)
+            w_dealt_plane[:].rearrange("p (t m) -> p t m", t=PACK),
+            w_plane[:].rearrange("p (m t) -> p t m", t=PACK),
         )
-        wp_w = tile("wp_w", [P, R], U32)
+        w_dealt = tile("w_dealt", [P, R], U32)
         nc.scalar.copy(
-            wp_w[:].rearrange("p (t c i) -> p c t i", t=4, i=4), w_w[:].rearrange("p (c i t) -> p c t i", t=4, i=4)
+            w_dealt[:].rearrange("p (t c i) -> p c t i", t=PACK, i=RUN),
+            w_raw[:].rearrange("p (c i t) -> p c t i", t=PACK, i=RUN),
         )
-        gains = tile("gains", [P, 16], F32, tag="w_st")
-        sb_t = gains[:, 0:4]
-        sa_t = gains[:, 8:12]
-        nc.sync.dma_start(sb_t, sb.rearrange("(p t) o -> p (t o)", t=4))
-        nc.sync.dma_start(sa_t, sa.rearrange("(p t) o -> p (t o)", t=4))
-        out_w = tile("out_w", [P, 2 * N], U32, tag="w_w")
-        ws_w = out_w[:, 0:N]
-        wb_w = out_w[:, N : 2 * N]
-        nc.sync.dma_start(ws_w.bitcast(I32), fp8_words(ws_words).bitcast(I32))
-        nc.sync.dma_start(wb_w.bitcast(I32), fp8_words(wb_words).bitcast(I32))
-        out_pl = tile("out_pl", [P, 2 * N], U8, tag="w_pl")
-        ws_pl = out_pl[:, 0:N]
-        wb_pl = out_pl[:, N : 2 * N]
-        nc.vector.memset(out_pl[:].bitcast(I32), 0)
-        load_plane(nc.sync, ws_pl, ws_scales)
-        load_plane(nc.sync, wb_pl, wb_scales)
 
-        xo_g = tile("xo_g", [P, J], U16)
-        xo_gs = tile("xo_gs", [P, J], U8)
-        nc.vector.tensor_copy(xo_g[:], xo_w[:].indirect(l2[:]))
-        nc.vector.tensor_copy(xo_gs[:], xo_pl[:].indirect(l2[:]))
-        picked = tile("picked", [P, J + O], U32, tag="xo_pl")
-        xt_g = picked[:, 0:J]
-        x6_g = picked[:, J : J + O]
-        xt_gs = tile("xt_gs", [P, J], U8)
-        x6_gs = tile("x6_gs", [P, O], U8)
-        nc.vector.tensor_copy(xt_g, xt_w[:].indirect(l1[:]))
-        nc.vector.tensor_copy(xt_gs[:], xt_pl[:].indirect(l1[:]))
-        nc.vector.tensor_copy(x6_g, xt_w[:].indirect(l6[:]))
-        nc.vector.tensor_copy(x6_gs[:], xt_pl[:].indirect(l6[:]))
+        row_weights = tile("row_weights", [P, 16], F32, tag="w_rows")
+        sb_cols = row_weights[:, 0:PACK]
+        sa_cols = row_weights[:, 8 : 8 + PACK]
+        nc.sync.dma_start(sb_cols, sb.rearrange("(p t) o -> p (t o)", t=PACK))
+        nc.sync.dma_start(sa_cols, sa.rearrange("(p t) o -> p (t o)", t=PACK))
+        out_stage_words = tile("out_stage_words", [P, 2 * N], U32, tag="w_raw")
+        ws_codes = out_stage_words[:, 0:N]
+        wb_codes = out_stage_words[:, N : 2 * N]
+        nc.sync.dma_start(ws_codes.bitcast(I32), fp8_words(ws_words).bitcast(I32))
+        nc.sync.dma_start(wb_codes.bitcast(I32), fp8_words(wb_words).bitcast(I32))
+        out_stage_planes = tile("out_stage_planes", [P, 2 * N], U8, tag="w_plane")
+        ws_plane = out_stage_planes[:, 0:N]
+        wb_plane = out_stage_planes[:, N : 2 * N]
+        nc.vector.memset(out_stage_planes[:].bitcast(I32), 0)
+        load_plane(ws_plane, ws_scales)
+        load_plane(wb_plane, wb_scales)
 
-        def first_stage(bank, t, codes, scales):
+        xo_codes = tile("xo_codes", [P, J], U16)
+        xo_picked_plane = tile("xo_picked_plane", [P, J], U8)
+        nc.vector.tensor_copy(xo_codes[:], xo_table[:].indirect(list2[:]))
+        nc.vector.tensor_copy(xo_picked_plane[:], xo_plane[:].indirect(list2[:]))
+        xt_picked = tile("xt_picked", [P, J + O], U32, tag="xo_plane")
+        xt_codes = xt_picked[:, 0:J]
+        short_codes = xt_picked[:, J : J + O]
+        xt_picked_plane = tile("xt_picked_plane", [P, J], U8)
+        short_plane = tile("short_plane", [P, O], U8)
+        nc.vector.tensor_copy(xt_codes, xt_table[:].indirect(list1[:]))
+        nc.vector.tensor_copy(xt_picked_plane[:], xt_plane[:].indirect(list1[:]))
+        nc.vector.tensor_copy(short_codes, xt_table[:].indirect(list6[:]))
+        nc.vector.tensor_copy(short_plane[:], xt_plane[:].indirect(list6[:]))
+
+        def first_stage(bank, t, codes, plane):
             acc = psum.tile([P, J], F32, name="acc", tag=f"bank{bank}")
             cols = slice(t * P, (t + 1) * P)
             nc.tensor.matmul_mx(
-                out=acc[:], lhsT=wp_w[:, cols].bitcast(E5M2), lhsT_scale=wp_pl[:, cols],
-                rhs=codes, rhs_scale=scales, start=True, stop=True,
+                out=acc[:], lhsT=w_dealt[:, cols].bitcast(E5M2), lhsT_scale=w_dealt_plane[:, cols],
+                rhs=codes, rhs_scale=plane, start=True, stop=True,
             )
             return acc
 
-        b_ps = [first_stage(t, t, xo_g[:].bitcast(E2M1), xo_gs[:]) for t in range(4)]
-        a_ps = [first_stage(4 + t, t, xt_g.bitcast(E4M3), xt_gs[:]) for t in range(4)]
+        b_psum = [first_stage(t, t, xo_codes[:].bitcast(E2M1), xo_picked_plane[:]) for t in range(PACK)]
+        a_psum = [first_stage(PACK + t, t, xt_codes.bitcast(E4M3), xt_picked_plane[:]) for t in range(PACK)]
 
-        b_sb = [tile(f"b_sb{t}", [P, J], F32) for t in range(3)]
-        a_sb = [tile(f"a_sb{t}", [P, J], F32) for t in range(4)]
-        a3 = tile("a3", [P, 4, O], F32)
-        a4 = tile("a4", [P, 4, O], F32)
-        b5 = tile("b5", [P, 4, O], F32)
-        top = tile("top", [P, 4, O], F32)
+        b_rows = [tile(f"b_rows{t}", [P, J], F32) for t in range(LAST)]
+        a_rows = [tile(f"a_rows{t}", [P, J], F32) for t in range(PACK)]
+        a_scaled = tile("a_scaled", [P, PACK, O], F32)
+        a_plain = tile("a_plain", [P, PACK, O], F32)
+        b_scaled = tile("b_scaled", [P, PACK, O], F32)
+        larger = tile("larger", [P, PACK, O], F32)
 
-        def look(dst, window, lst, scale):
+        def scaled_pick(dst, window, lst, scale):
             nc.scalar.activation(out=dst, in_=window[:].indirect(lst[:]), func=COPY, scale=scale)
 
-        for t in range(4):
-            if t < 3:
-                nc.scalar.activation(out=b_sb[t][:], in_=b_ps[t][:], func=COPY)
+        for t in range(PACK):
+            if t < LAST:
+                nc.scalar.activation(out=b_rows[t][:], in_=b_psum[t][:], func=COPY)
             if t > 0:
-                look(b5[:, t - 1, :], b_sb[t - 1], l5, sb_t[:, t - 1 : t])
+                scaled_pick(b_scaled[:, t - 1, :], b_rows[t - 1], list5, sb_cols[:, t - 1 : t])
 
-        y_ps = [psum.tile([P, O], F32, name="y_ps", tag=f"bank{h}") for h in range(2)]
-        for h in range(2):
-            cols = slice(h * P, (h + 1) * P)
+        out_halves = [slice(h * P, (h + 1) * P) for h in range(N // P)]
+        y_psum = [psum.tile([P, O], F32, name="y_psum", tag=f"bank{h}") for h in range(N // P)]
+        for acc, cols in zip(y_psum, out_halves):
             nc.tensor.matmul_mx(
-                out=y_ps[h][:], lhsT=ws_w[:, cols].bitcast(E5M2), lhsT_scale=ws_pl[:, cols],
-                rhs=x6_g.bitcast(E4M3), rhs_scale=x6_gs[:], start=True, stop=False,
+                out=acc[:], lhsT=ws_codes[:, cols].bitcast(E5M2), lhsT_scale=ws_plane[:, cols],
+                rhs=short_codes.bitcast(E4M3), rhs_scale=short_plane[:], start=True, stop=False,
             )
 
-        for t in range(4):
-            nc.vector.tensor_copy(a_sb[t][:], a_ps[t][:])
-            look(a3[:, t, :], a_sb[t], l3, sa_t[:, t : t + 1])
-        for t in range(3):
-            nc.vector.tensor_copy(a4[:, t, :], a_sb[t][:].indirect(l4[:]))
-        b_last = tile("b_last", [P, J], F32, tag="a_sb0")
-        nc.scalar.activation(out=b_last[:], in_=b_ps[3][:], func=COPY)
-        nc.scalar.activation(out=a4[:, 3, :], in_=a_sb[3][:].indirect(l4[:]), func=COPY)
-        look(b5[:, 3, :], b_last, l5, sb_t[:, 3:4])
-        nc.vector.tensor_tensor(top[:, 0:3, :], a3[:, 0:3, :], a4[:, 0:3, :], ALU.max)
-        nc.vector.tensor_tensor(top[:, 3, :], a3[:, 3, :], a4[:, 3, :], ALU.max)
+        for t in range(PACK):
+            nc.vector.tensor_copy(a_rows[t][:], a_psum[t][:])
+            scaled_pick(a_scaled[:, t, :], a_rows[t], list3, sa_cols[:, t : t + 1])
+        for t in range(LAST):
+            nc.vector.tensor_copy(a_plain[:, t, :], a_rows[t][:].indirect(list4[:]))
+        b_last = tile("b_last", [P, J], F32, tag="a_rows0")
+        nc.scalar.activation(out=b_last[:], in_=b_psum[LAST][:], func=COPY)
+        nc.scalar.activation(out=a_plain[:, LAST, :], in_=a_rows[LAST][:].indirect(list4[:]), func=COPY)
+        scaled_pick(b_scaled[:, LAST, :], b_last, list5, sb_cols[:, LAST : LAST + 1])
+        nc.vector.tensor_tensor(larger[:, 0:LAST, :], a_scaled[:, 0:LAST, :], a_plain[:, 0:LAST, :], ALU.max)
+        nc.vector.tensor_tensor(larger[:, LAST, :], a_scaled[:, LAST, :], a_plain[:, LAST, :], ALU.max)
 
-        hid = tile("hid", [P, O, 4], BF16)
-        hid_q = tile("hid_q", [P, O], U32)
-        hid_s = tile("hid_s", [P, O], U8)
-        halves = [slice(0, O // 2), slice(O // 2, O)]
-        for cols in halves:
+        hid = tile("hid", [P, O, PACK], BF16)
+        hid_codes = tile("hid_codes", [P, O], U32)
+        hid_plane = tile("hid_plane", [P, O], U8)
+        place_halves = [slice(0, O // 2), slice(O // 2, O)]
+        for places in place_halves:
             nc.vector.tensor_tensor(
-                hid[:, cols, :].rearrange("p (c i) t -> p c t i", i=4),
-                top[:, :, cols].rearrange("p t (c i) -> p c t i", i=4),
-                b5[:, :, cols].rearrange("p t (c i) -> p c t i", i=4),
+                hid[:, places, :].rearrange("p (c i) t -> p c t i", i=RUN),
+                larger[:, :, places].rearrange("p t (c i) -> p c t i", i=RUN),
+                b_scaled[:, :, places].rearrange("p t (c i) -> p c t i", i=RUN),
                 ALU.subtract,
             )
-        for cols in halves:
+        for places in place_halves:
             nc.vector.quantize_mx(
-                out=hid_q[:, cols].bitcast(E4M3), scales=hid_s[:, cols],
-                in_=hid[:, cols, :].rearrange("p o t -> p (o t)"),
+                out=hid_codes[:, places].bitcast(E4M3), scales=hid_plane[:, places],
+                in_=hid[:, places, :].rearrange("p o t -> p (o t)"),
             )
 
-        y_sb = [tile(f"y{h}", [P, O], F32) for h in range(2)]
-        for h in range(2):
-            cols = slice(h * P, (h + 1) * P)
+        y_rows = [tile(f"y_rows{h}", [P, O], F32) for h in range(N // P)]
+        for acc, cols in zip(y_psum, out_halves):
             nc.tensor.matmul_mx(
-                out=y_ps[h][:], lhsT=wb_w[:, cols].bitcast(E5M2), lhsT_scale=wb_pl[:, cols],
-                rhs=hid_q[:].bitcast(E4M3), rhs_scale=hid_s[:], start=False, stop=True,
+                out=acc[:], lhsT=wb_codes[:, cols].bitcast(E5M2), lhsT_scale=wb_plane[:, cols],
+                rhs=hid_codes[:].bitcast(E4M3), rhs_scale=hid_plane[:], start=False, stop=True,
             )
-        nc.vector.tensor_copy(y_sb[0][:], y_ps[0][:])
-        nc.sync.dma_start(out[0:P, :], y_sb[0][:])
-        nc.scalar.copy(y_sb[1][:], y_ps[1][:])
-        nc.scalar.dma_start(out[P : 2 * P, :], y_sb[1][:])
+        nc.vector.tensor_copy(y_rows[0][:], y_psum[0][:])
+        nc.sync.dma_start(out[out_halves[0], :], y_rows[0][:])
+        nc.scalar.copy(y_rows[1][:], y_psum[1][:])
+        nc.scalar.dma_start(out[out_halves[1], :], y_rows[1][:])

from contextlib import ExitStack

import concourse.mybir as mybir

K, T, Z, J, R, O, N = 512, 1024, 1024, 256, 512, 128, 256
FLOPS = 2 * K * R * J * 2 + 2 * R * N * O + 2 * K * N * O

F32 = mybir.dt.float32
BF16 = mybir.dt.bfloat16
I32 = mybir.dt.int32
U32 = mybir.dt.uint32
U16 = mybir.dt.uint16
U8 = mybir.dt.uint8
E4M3 = mybir.dt.float8_e4m3fn_x4
E5M2 = mybir.dt.float8_e5m2_x4
E2M1 = mybir.dt.float4_e2m1fn_x4
ALU = mybir.AluOpType
COPY = mybir.ActivationFunctionType.Copy

P = 128
PACK = 4
QUADS = 4
LAST = PACK - 1
RUN = 4


def tile_list_overthird_oneforboth_further_plain_kernel(
    tc, xt_words, xt_scales, xo_words, xo_scales, w_words, w_scales, sa, sb,
    wb_words, wb_scales, ws_words, ws_scales, offs, offs2, offs3, offs4, offs5, offs6, out,
):
    nc = tc.nc
    with ExitStack() as ctx:
        sbuf = ctx.enter_context(tc.tile_pool(name="sbuf", bufs=1))
        psum = ctx.enter_context(tc.psum_pool(name="psum", bufs=1))

        def tile(name, shape, dtype, tag=None):
            return sbuf.tile(shape, dtype, name=name, tag=tag or name, align_bytes=64)

        def load_list(name, src):
            lst = tile(name, list(src.shape), U16)
            nc.sync.dma_start(lst[:], src)
            return lst

        def load_words(queue, name, src, dtype, cols):
            words = tile(name, [P, cols], dtype)
            queue.dma_start(words[:].bitcast(I32), src.bitcast(I32))
            return words

        def fp8_words(src):
            return src[0].rearrange("p n t -> p (n t)")

        def load_plane(plane, src):
            for q in range(QUADS):
                rows = src[0, 4 * q : 4 * q + 4, :]
                nc.sync.dma_start(plane[32 * q : 32 * q + 4, :].bitcast(I32), rows.bitcast(I32))

        xo_plane = tile("xo_plane", [P, Z], U8)
        w_rows = tile("w_rows", [4, QUADS, R // 4], I32)
        w_plane = tile("w_plane", [P, R], U8)
        xt_plane = tile("xt_plane", [P, T], U8)
        nc.vector.memset(xo_plane[:].bitcast(I32), 0)
        nc.vector.memset(xt_plane[:].bitcast(I32), 0)
        nc.vector.memset(w_plane[:].bitcast(I32), 0)

        w_raw = load_words(nc.gpsimd, "w_raw", fp8_words(w_words), U32, R)
        xt_table = load_words(nc.gpsimd, "xt_table", fp8_words(xt_words), U32, T)
        nc.scalar.dma_start(w_rows[:], w_scales[0].bitcast(I32).rearrange("(q i) n -> i q n", q=QUADS))
        list2 = load_list("list2", offs2)
        list1 = load_list("list1", offs)
        list5 = load_list("list5", offs5)
        xo_table = load_words(nc.sync, "xo_table", xo_words[0], U16, Z)
        list6 = load_list("list6", offs6)
        list3 = load_list("list3", offs3)
        list4 = load_list("list4", offs4)
        load_plane(xo_plane, xo_scales)
        load_plane(xt_plane, xt_scales)

        for q in range(QUADS):
            nc.vector.tensor_copy(w_plane[32 * q : 32 * q + 4, :].bitcast(I32), w_rows[:, q, :])
        w_dealt_plane = tile("w_dealt_plane", [P, R], U8)
        nc.vector.tensor_copy(
            w_dealt_plane[:].rearrange("p (t m) -> p t m", t=PACK),
            w_plane[:].rearrange("p (m t) -> p t m", t=PACK),
        )
        w_dealt = tile("w_dealt", [P, R], U32)
        nc.scalar.copy(
            w_dealt[:].rearrange("p (t c i) -> p c t i", t=PACK, i=RUN),
            w_raw[:].rearrange("p (c i t) -> p c t i", t=PACK, i=RUN),
        )

        row_weights = tile("row_weights", [P, 16], F32, tag="w_rows")
        sb_cols = row_weights[:, 0:PACK]
        sa_cols = row_weights[:, 8 : 8 + PACK]
        nc.sync.dma_start(sb_cols, sb.rearrange("(p t) o -> p (t o)", t=PACK))
        nc.sync.dma_start(sa_cols, sa.rearrange("(p t) o -> p (t o)", t=PACK))
        out_stage_words = tile("out_stage_words", [P, 2 * N], U32, tag="w_raw")
        ws_codes = out_stage_words[:, 0:N]
        wb_codes = out_stage_words[:, N : 2 * N]
        nc.sync.dma_start(ws_codes.bitcast(I32), fp8_words(ws_words).bitcast(I32))
        nc.sync.dma_start(wb_codes.bitcast(I32), fp8_words(wb_words).bitcast(I32))
        out_stage_planes = tile("out_stage_planes", [P, 2 * N], U8, tag="w_plane")
        ws_plane = out_stage_planes[:, 0:N]
        wb_plane = out_stage_planes[:, N : 2 * N]
        nc.vector.memset(out_stage_planes[:].bitcast(I32), 0)
        load_plane(ws_plane, ws_scales)
        load_plane(wb_plane, wb_scales)

        xo_codes = tile("xo_codes", [P, J], U16)
        xo_picked_plane = tile("xo_picked_plane", [P, J], U8)
        nc.vector.tensor_copy(xo_codes[:], xo_table[:].indirect(list2[:]))
        nc.vector.tensor_copy(xo_picked_plane[:], xo_plane[:].indirect(list2[:]))
        xt_picked = tile("xt_picked", [P, J + O], U32, tag="xo_plane")
        xt_codes = xt_picked[:, 0:J]
        short_codes = xt_picked[:, J : J + O]
        xt_picked_plane = tile("xt_picked_plane", [P, J], U8)
        short_plane = tile("short_plane", [P, O], U8)
        nc.vector.tensor_copy(xt_codes, xt_table[:].indirect(list1[:]))
        nc.vector.tensor_copy(xt_picked_plane[:], xt_plane[:].indirect(list1[:]))
        nc.vector.tensor_copy(short_codes, xt_table[:].indirect(list6[:]))
        nc.vector.tensor_copy(short_plane[:], xt_plane[:].indirect(list6[:]))

        def first_stage(bank, t, codes, plane):
            acc = psum.tile([P, J], F32, name="acc", tag=f"bank{bank}")
            cols = slice(t * P, (t + 1) * P)
            nc.tensor.matmul_mx(
                out=acc[:], lhsT=w_dealt[:, cols].bitcast(E5M2), lhsT_scale=w_dealt_plane[:, cols],
                rhs=codes, rhs_scale=plane, start=True, stop=True,
            )
            return acc

        b_psum = [first_stage(t, t, xo_codes[:].bitcast(E2M1), xo_picked_plane[:]) for t in range(PACK)]
        a_psum = [first_stage(PACK + t, t, xt_codes.bitcast(E4M3), xt_picked_plane[:]) for t in range(PACK)]

        b_rows = [tile(f"b_rows{t}", [P, J], F32) for t in range(LAST)]
        a_rows = [tile(f"a_rows{t}", [P, J], F32) for t in range(PACK)]
        a_scaled = tile("a_scaled", [P, PACK, O], F32)
        a_plain = tile("a_plain", [P, PACK, O], F32)
        b_scaled = tile("b_scaled", [P, PACK, O], F32)
        larger = tile("larger", [P, PACK, O], F32)

        def scaled_pick(dst, window, lst, scale):
            nc.scalar.activation(out=dst, in_=window[:].indirect(lst[:]), func=COPY, scale=scale)

        for t in range(PACK):
            if t < LAST:
                nc.scalar.activation(out=b_rows[t][:], in_=b_psum[t][:], func=COPY)
            if t > 0:
                scaled_pick(b_scaled[:, t - 1, :], b_rows[t - 1], list5, sb_cols[:, t - 1 : t])

        out_halves = [slice(h * P, (h + 1) * P) for h in range(N // P)]
        y_psum = [psum.tile([P, O], F32, name="y_psum", tag=f"bank{h}") for h in range(N // P)]
        for acc, cols in zip(y_psum, out_halves):
            nc.tensor.matmul_mx(
                out=acc[:], lhsT=ws_codes[:, cols].bitcast(E5M2), lhsT_scale=ws_plane[:, cols],
                rhs=short_codes.bitcast(E4M3), rhs_scale=short_plane[:], start=True, stop=False,
            )

        for t in range(PACK):
            nc.vector.tensor_copy(a_rows[t][:], a_psum[t][:])
            scaled_pick(a_scaled[:, t, :], a_rows[t], list3, sa_cols[:, t : t + 1])
        for t in range(LAST):
            nc.vector.tensor_copy(a_plain[:, t, :], a_rows[t][:].indirect(list4[:]))
        b_last = tile("b_last", [P, J], F32, tag="a_rows0")
        nc.scalar.activation(out=b_last[:], in_=b_psum[LAST][:], func=COPY)
        nc.scalar.activation(out=a_plain[:, LAST, :], in_=a_rows[LAST][:].indirect(list4[:]), func=COPY)
        scaled_pick(b_scaled[:, LAST, :], b_last, list5, sb_cols[:, LAST : LAST + 1])
        nc.vector.tensor_tensor(larger[:, 0:LAST, :], a_scaled[:, 0:LAST, :], a_plain[:, 0:LAST, :], ALU.max)
        nc.vector.tensor_tensor(larger[:, LAST, :], a_scaled[:, LAST, :], a_plain[:, LAST, :], ALU.max)

        hid = tile("hid", [P, O, PACK], BF16)
        hid_codes = tile("hid_codes", [P, O], U32)
        hid_plane = tile("hid_plane", [P, O], U8)
        place_halves = [slice(0, O // 2), slice(O // 2, O)]
        for places in place_halves:
            nc.vector.tensor_tensor(
                hid[:, places, :].rearrange("p (c i) t -> p c t i", i=RUN),
                larger[:, :, places].rearrange("p t (c i) -> p c t i", i=RUN),
                b_scaled[:, :, places].rearrange("p t (c i) -> p c t i", i=RUN),
                ALU.subtract,
            )
        for places in place_halves:
            nc.vector.quantize_mx(
                out=hid_codes[:, places].bitcast(E4M3), scales=hid_plane[:, places],
                in_=hid[:, places, :].rearrange("p o t -> p (o t)"),
            )

        y_rows = [tile(f"y_rows{h}", [P, O], F32) for h in range(N // P)]
        for acc, cols in zip(y_psum, out_halves):
            nc.tensor.matmul_mx(
                out=acc[:], lhsT=wb_codes[:, cols].bitcast(E5M2), lhsT_scale=wb_plane[:, cols],
                rhs=hid_codes[:].bitcast(E4M3), rhs_scale=hid_plane[:], start=False, stop=True,
            )
        nc.vector.tensor_copy(y_rows[0][:], y_psum[0][:])
        nc.sync.dma_start(out[out_halves[0], :], y_rows[0][:])
        nc.scalar.copy(y_rows[1][:], y_psum[1][:])
        nc.scalar.dma_start(out[out_halves[1], :], y_rows[1][:])
